import numpy as np
import ml_dtypes


def mxq(x, axis, fmt="e4m3"):
    dtype, down = {"e4m3": (ml_dtypes.float8_e4m3fn, 7), "e5m2": (ml_dtypes.float8_e5m2, 14)}[fmt]
    v = np.moveaxis(np.asarray(x, np.float32).astype(ml_dtypes.bfloat16).astype(np.float64), axis, -1)
    blocks = v.reshape(v.shape[:-1] + (-1, 32))
    amax = np.abs(blocks).max(-1, keepdims=True)
    byte = np.maximum(np.where(amax > 0, np.frexp(amax)[1] - 1 + 127, 0) - down, 1)
    scale = np.exp2(byte - 127.0)
    codes = (blocks / scale).astype(np.float32).astype(dtype).astype(np.float64)
    return np.moveaxis((codes * scale).reshape(v.shape), -1, axis)


WIDE = False


def mx_kscale(k):
    if not WIDE:
        return np.ones(k)
    levels = np.array([10, -10, 5, -5, 0])
    if k % 512:
        return np.exp2(np.random.permutation(np.resize(levels, k // 32))).repeat(32)
    a = np.empty((k // 512, 16))
    for p in range(k // 512):
        a[p, :8] = np.random.permutation(np.resize(levels, 8))
        for g in range(8):
            far = levels[np.abs(levels - a[p, g]) >= 10]
            a[p, g + 8] = far[np.random.randint(len(far))]
    return np.exp2(a.ravel()).repeat(32)


def f64(x):
    return np.asarray(x).astype(np.float64)


def striped(idx):
    return np.tile(idx.reshape(-1, 16).T, (8, 1)).astype(np.uint16)


def unstriped(offs):
    return offs[:16].T.reshape(-1).astype(np.int64)


def striped8(idx):
    return np.concatenate([x.reshape(-1, 16).T for x in idx]).astype(np.uint16)


def runs(offs, k):
    lists = np.stack([offs[16 * r : 16 * r + 16].T.reshape(-1) for r in range(8)]).astype(np.int64)
    return lists[np.arange(k) % 512 // 64]


def pack_weight(w):
    k, n = w.shape
    w = f64(np.asarray(w, np.float32).astype(ml_dtypes.bfloat16)).reshape(k // 32, 32, n)
    amax = np.abs(w).max(1)
    byte = np.clip(np.where(amax > 0, np.frexp(amax)[1] - 1 + 127 - 7, 1), 1, 254)
    scaled = (w * np.exp2(127.0 - byte)[:, None, :]).reshape(k, n).astype(np.float32)
    words = np.ascontiguousarray(scaled.reshape(k // 512, 128, 4, n).transpose(0, 1, 3, 2)).astype(ml_dtypes.float8_e4m3fn).view(np.uint8)
    return words, np.ascontiguousarray(byte.astype(np.uint8).reshape(k // 512, 16, n))


def unpack_weight(words, scales):
    g, p, n, _ = words.shape
    vals = np.ascontiguousarray(words).view(ml_dtypes.float8_e4m3fn).astype(np.float64) * np.repeat(np.exp2(scales.astype(np.float64) - 127.0), 8, axis=1)[..., None]
    return vals.transpose(0, 1, 3, 2).reshape(g * 512, n)


def sigmoid(v):
    return 1.0 / (1.0 + np.exp(-np.maximum(v, -700.0)))

def planes(y):
    n, m = y.shape
    v = y.astype(np.float32).astype(ml_dtypes.bfloat16).astype(np.float64).reshape(n // 32, 32, m)
    top = np.abs(v).max(1)
    byte = np.clip(np.where(top > 0, np.frexp(top)[1] - 1 + 127 - 7, 1), 1, 254)
    codes = (v * np.exp2(127.0 - byte)[:, None, :]).reshape(n, m).astype(np.float32).astype(ml_dtypes.float8_e4m3fn).view(np.uint8)
    words = codes.reshape(n // 512, 128, 4, m).transpose(0, 1, 3, 2)
    return np.ascontiguousarray(words), np.ascontiguousarray(byte.astype(np.uint8).reshape(n // 512, 16, m))


K, T, S, N, G, H, W = 512, 1024, 256, 512, 2048, 512, 128


def setup_inputs():
    n = np.random.standard_normal
    s = mx_kscale(K)[:, None]
    u = mx_kscale(K)
    packed_xT = pack_weight(n((K, T)) * s)
    packed_dT = pack_weight(n((K, G)) / s)
    packed_w1 = pack_weight(n((H, N)) / np.sqrt(2 * H) / u[:, None])
    packed_w2 = pack_weight(n((K, N)) / np.sqrt(2 * K) / s)
    perm = np.random.permutation(S)
    return {
        "x_words": packed_xT[0],
        "x_scales": packed_xT[1],
        "d_words": packed_dT[0],
        "d_scales": packed_dT[1],
        "gn": (np.random.uniform(0.5, 1.5, (H, 1)) * u[:, None]).astype(np.float32),
        "w1_words": packed_w1[0],
        "w1_scales": packed_w1[1],
        "w2_words": packed_w2[0],
        "w2_scales": packed_w2[1],
        "offs": striped(np.random.permutation(T)[:S]),
        "k1": striped8(np.random.randint(0, G, (8, H))),
        "n1": striped(perm[:W]),
        "n2": striped(perm[W:]),
        "two": striped(np.random.permutation(T)[:S]),
        "n3": striped8(np.stack([np.random.permutation(S) for _ in range(8)])),
        "n4": striped8(np.stack([np.random.permutation(S) for _ in range(8)])),
    }


def reference(x_words, x_scales, d_words, d_scales, gn, w1_words, w1_scales, w2_words, w2_scales, offs, k1, n1, n2, two, n3, n4):
    d_k1 = unpack_weight(d_words, d_scales)[np.arange(K)[:, None], runs(k1, K)]
    xq = unpack_weight(x_words, x_scales)[:, unstriped(offs)]
    h = 0.0625 * (d_k1.T @ xq)
    pa = h[:, unstriped(n1)]
    pb = h[:, unstriped(n2)]
    ra = np.maximum(pa, pb)
    ds = h.copy()
    ds[:, unstriped(n1)] = ra
    z = f64(gn) * ds
    x_two = unpack_weight(x_words, x_scales)[:, unstriped(two)]
    h2 = unpack_weight(w1_words, w1_scales).T @ mxq(z, 0, "e4m3") + unpack_weight(w2_words, w2_scales).T @ x_two
    st = h2[np.arange(N)[:, None], runs(n3, N)] - h2
    out_0 = h2 * (sigmoid(st[np.arange(N)[:, None], runs(n4, N)]))
    return (out_0,) + planes(out_0)

@@ -1,0 +1,189 @@
+from contextlib import ExitStack
+
+import concourse.mybir as mybir
+
+K, T, S, N, G, H, W = 512, 1024, 256, 512, 2048, 512, 128
+P = 128
+PACK = 4
+HALF = S // 2
+
+F32 = mybir.dt.float32
+BF16 = mybir.dt.bfloat16
+I32 = mybir.dt.int32
+U32 = mybir.dt.uint32
+U16 = mybir.dt.uint16
+U8 = mybir.dt.uint8
+FP8X4 = mybir.dt.float8_e4m3fn_x4
+ALU = mybir.AluOpType
+ACT = mybir.ActivationFunctionType
+
+FLOPS = 2 * K * H * S + 2 * H * N * S + 2 * K * N * S
+
+
+def tile_picked_pqmixfillhopd_none_po_kernel(
+    tc, x_words, x_scales, d_words, d_scales, gn, w1_words, w1_scales, w2_words, w2_scales,
+    offs, k1, n1, n2, two, n3, n4, out_0, out_1, out_2,
+):
+    nc = tc.nc
+
+    def words_in_hbm(words):
+        return words[0].rearrange("p n t -> p (n t)").bitcast(I32)
+
+    with ExitStack() as ctx:
+        lists = ctx.enter_context(tc.tile_pool(name="lists", bufs=1))
+        keep = ctx.enter_context(tc.tile_pool(name="keep", bufs=1))
+        psum = ctx.enter_context(tc.psum_pool(name="psum", bufs=1))
+
+        def list_tile(name, source):
+            return lists.tile(list(source.shape), U16, name=name)
+
+        def sb(name, shape, dtype, tag=None):
+            return keep.tile(shape, dtype, name=name, tag=tag or name, align_bytes=64)
+
+        k1_t, offs_t, two_t = list_tile("k1_t", k1), list_tile("offs_t", offs), list_tile("two_t", two)
+        n1_t, n2_t = list_tile("n1_t", n1), list_tile("n2_t", n2)
+        n3_t, n4_t = list_tile("n3_t", n3), list_tile("n4_t", n4)
+
+        d_sc, x_sc = sb("d_sc", [P, G], U8), sb("x_sc", [P, T], U8, tag="x_sc_then_words")
+        d_w, x_w = sb("d_w", [P, G], U32, tag="d_w_then_w_w"), sb("x_w", [P, T], U32)
+        gain = sb("gain", [P, PACK], F32)
+        picked_sc = sb("picked_sc", [P, H + 2 * S], U8, tag="picked_then_w_sc")
+        placed_sc = sb("placed_sc", [P, H + 2 * S], U8)
+
+        nc.vector.memset(d_sc[:].bitcast(I32), 0)
+        nc.vector.memset(x_sc[:].bitcast(I32), 0)
+        nc.gpsimd.memset(placed_sc[:].bitcast(I32), 0)
+
+        nc.gpsimd.dma_start(gain[:], gn.rearrange("(p t) o -> p (t o)", t=PACK))
+        nc.scalar.dma_start(d_sc[0:P:8, :].bitcast(I32), d_scales[0].bitcast(I32))
+        nc.scalar.dma_start(x_sc[0:P:8, :].bitcast(I32), x_scales[0].bitcast(I32))
+        for list_t, source in ((k1_t, k1), (offs_t, offs), (two_t, two), (n1_t, n1), (n2_t, n2)):
+            nc.sync.dma_start(list_t[:], source)
+        nc.sync.dma_start(d_w[:].bitcast(I32), words_in_hbm(d_words))
+        nc.sync.dma_start(x_w[:].bitcast(I32), words_in_hbm(x_words))
+        nc.sync.dma_start(n3_t[:], n3)
+        nc.sync.dma_start(n4_t[:], n4)
+
+        nc.vector.tensor_copy(picked_sc[:, 0:H], d_sc[:].indirect(k1_t[:]))
+        nc.vector.tensor_copy(picked_sc[:, H : H + S], x_sc[:].indirect(offs_t[:]))
+        nc.vector.tensor_copy(picked_sc[:, H + S :], x_sc[:].indirect(two_t[:]))
+        for r in range(4):
+            queue = nc.scalar if r % 2 else nc.sync
+            queue.dma_start(placed_sc[r:P:32, :].bitcast(I32), picked_sc[8 * r : P : 32, :].bitcast(I32))
+
+        picked_w = sb("picked_w", [P, H + 2 * S], U32, tag="x_sc_then_words")
+        d_picked, xq_w, x2_w = picked_w[:, 0:H], picked_w[:, H : H + S], picked_w[:, H + S :]
+        d_dealt, d_dealt_sc = sb("d_dealt", [P, H], U32), sb("d_dealt_sc", [P, H], U8)
+        nc.vector.tensor_copy(d_picked, d_w[:].indirect(k1_t[:]))
+        nc.vector.tensor_copy(xq_w, x_w[:].indirect(offs_t[:]))
+        nc.vector.tensor_copy(
+            d_dealt[:].bitcast(I32).rearrange("p (t m) -> p t m", t=PACK),
+            d_picked.bitcast(I32).rearrange("p (m t) -> p t m", t=PACK),
+        )
+        for u in range(2):
+            nc.vector.tensor_copy(
+                d_dealt_sc[:].rearrange("p (t m) -> p t m", t=PACK)[:, 2 * u : 2 * u + 2, :],
+                placed_sc[:, 0:H].rearrange("p (m t) -> p t m", t=PACK)[:, 2 * u : 2 * u + 2, :],
+            )
+
+        w_w = sb("w_w", [P, 2 * N], U32, tag="d_w_then_w_w")
+        nc.sync.dma_start(w_w[:, N:].bitcast(I32), words_in_hbm(w2_words))
+        nc.sync.dma_start(w_w[:, 0:N].bitcast(I32), words_in_hbm(w1_words))
+        w_sc = sb("w_sc", [P, N], U8, tag="picked_then_w_sc")
+        nc.gpsimd.memset(w_sc[:].bitcast(I32), 0)
+        for which, scales in enumerate((w1_scales, w2_scales)):
+            for q in range(4):
+                first = 32 * q + 4 * which
+                nc.sync.dma_start(
+                    w_sc[first : first + 4, :].bitcast(I32), scales[0, 4 * q : 4 * q + 4, :].bitcast(I32)
+                )
+
+        h_ps = [psum.tile([P, S], F32, name="h_ps%d" % t) for t in range(PACK)]
+        h2_ps = [psum.tile([P, S], F32, name="h2_ps%d" % t) for t in range(PACK)]
+        for t in range(PACK):
+            cols = slice(P * t, P * (t + 1))
+            nc.tensor.matmul_mx(
+                out=h_ps[t][:], lhsT=d_dealt[:, cols].bitcast(FP8X4), lhsT_scale=d_dealt_sc[:, cols],
+                rhs=xq_w.bitcast(FP8X4), rhs_scale=placed_sc[:, H : H + S], start=True, stop=True,
+            )
+
+        ds = [sb("ds%d" % t, [P, S], F32) for t in range(PACK)]
+        ra = [sb("ra%d" % t, [P, W], F32) for t in range(PACK)]
+        for t in range(PACK):
+            pa, pb = sb("pa%d" % t, [P, W], F32), sb("pb%d" % t, [P, W], F32)
+            if t == 0:
+                nc.scalar.copy(ds[t][:], h_ps[t][:])
+            else:
+                nc.vector.tensor_copy(ds[t][:], h_ps[t][:])
+            nc.scalar.activation(pa[:], ds[t][:].indirect(n1_t[:]), ACT.Copy)
+            nc.vector.tensor_copy(pb[:], ds[t][:].indirect(n2_t[:]))
+            nc.vector.tensor_tensor(ra[t][:], pa[:], pb[:], ALU.max)
+        for t in range(PACK):
+            nc.scalar.activation(ds[t][:].indirect(n1_t[:]), ra[t][:], ACT.Copy)
+        nc.vector.tensor_copy(x2_w, x_w[:].indirect(two_t[:]))
+        w_dealt, w_dealt_sc = sb("w_dealt", [P, 2 * N], U32), sb("w_dealt_sc", [P, N], U8)
+        for first in (N, 0):
+            nc.vector.tensor_copy(
+                w_dealt[:, first : first + N].bitcast(I32).rearrange("p (t m) -> p t m", t=PACK),
+                w_w[:, first : first + N].bitcast(I32).rearrange("p (m t) -> p t m", t=PACK),
+            )
+        nc.vector.tensor_copy(
+            w_dealt_sc[:].rearrange("p (t m) -> p t m", t=PACK),
+            w_sc[:].rearrange("p (m t) -> p t m", t=PACK),
+        )
+
+        z_bf = sb("z_bf", [P, S, PACK], BF16, tag="picked_then_w_sc")
+        for t in range(PACK):
+            nc.vector.tensor_scalar(z_bf[:, :, t], ds[t][:], gain[:, t : t + 1], 0.0625, ALU.mult, ALU.mult)
+
+        z_w, z_sc = sb("z_w", [P, S], U32), sb("z_sc", [P, S], U8)
+        nc.gpsimd.memset(z_sc[:].bitcast(I32), 0)
+        nc.vector.quantize_mx(out=z_w[:].bitcast(FP8X4), scales=z_sc[:], in_=z_bf[:].rearrange("p j t -> p (j t)"))
+
+        for t in range(PACK):
+            cols = slice(P * t, P * (t + 1))
+            nc.tensor.matmul_mx(
+                out=h2_ps[t][:], lhsT=w_dealt[:, N + P * t : N + P * (t + 1)].bitcast(FP8X4),
+                lhsT_scale=w_dealt_sc[4:P, cols],
+                rhs=x2_w.bitcast(FP8X4), rhs_scale=placed_sc[:, H + S :], start=True, stop=False,
+            )
+        for t in range(PACK):
+            cols = slice(P * t, P * (t + 1))
+            nc.tensor.matmul_mx(
+                out=h2_ps[t][:], lhsT=w_dealt[:, cols].bitcast(FP8X4), lhsT_scale=w_dealt_sc[:, cols],
+                rhs=z_w[:].bitcast(FP8X4), rhs_scale=z_sc[:], start=False, stop=True,
+            )
+
+        st = []
+        for t in range(PACK):
+            h2, g3 = sb("h2_%d" % t, [P, 2 * S], F32), sb("g3_%d" % t, [P, S], F32)
+            st.append(sb("st%d" % t, [P, 2 * S], F32))
+            nc.gpsimd.memset(h2[:, S:], 0.0)
+            nc.gpsimd.memset(st[t][:, S:], 0.0)
+            if t == 0:
+                nc.scalar.copy(h2[:, 0:S], h2_ps[t][:])
+            else:
+                nc.vector.tensor_copy(h2[:, 0:S], h2_ps[t][:])
+            nc.scalar.activation(g3[:], h2[:].indirect(n3_t[:]), ACT.Copy)
+            nc.vector.tensor_tensor(st[t][:, 0:S], g3[:], h2_ps[t][:], ALU.subtract)
+
+        o_w, o_sc = sb("o_w", [P, S], U32), sb("o_sc", [P, S], U8)
+        out_rows = out_0.rearrange("(p t) j -> p t j", t=PACK)
+        out_words = out_1[0].rearrange("p n t -> p (n t)").bitcast(I32)
+        for u in range(2):
+            cols = slice(HALF * u, HALF * (u + 1))
+            res = sb("res%d" % u, [P, PACK, HALF], F32)
+            res_bf = sb("res_bf%d" % u, [P, HALF, PACK], BF16)
+            for t in range(PACK):
+                gate = sb("gate%d_%d" % (u, t), [P, HALF], F32)
+                nc.scalar.activation(gate[:], st[t][:].indirect(n4_t[:, 8 * u : 8 * u + 8]), ACT.Sigmoid)
+                nc.vector.tensor_tensor(res[:, t, :], gate[:], h2_ps[t][:, cols], ALU.mult)
+            nc.sync.dma_start(out_rows[:, :, cols], res[:])
+            nc.vector.tensor_copy(res_bf[:], res[:].rearrange("p t j -> p j t"))
+            nc.vector.quantize_mx(
+                out=o_w[:, cols].bitcast(FP8X4), scales=o_sc[:, cols], in_=res_bf[:].rearrange("p j t -> p (j t)")
+            )
+            nc.sync.dma_start(out_words[:, cols], o_w[:, cols].bitcast(I32))
+        for q in range(4):
+            queue = nc.scalar if q % 2 else nc.sync
+            queue.dma_start(out_2[0, 4 * q : 4 * q + 4, :].bitcast(I32), o_sc[32 * q : 32 * q + 4, :].bitcast(I32))

@@ -47,56 +47,64 @@ def tile_picked_pqmixfillhopd_none_po_kernel(
         d_sc, x_sc = sb("d_sc", [P, G], U8), sb("x_sc", [P, T], U8, tag="x_sc_then_words")
         d_w, x_w = sb("d_w", [P, G], U32, tag="d_w_then_w_w"), sb("x_w", [P, T], U32)
         gain = sb("gain", [P, PACK], F32)
-        picked_sc = sb("picked_sc", [P, H + 2 * S], U8, tag="picked_then_w_sc")
-        placed_sc = sb("placed_sc", [P, H + 2 * S], U8)
+        picked_sc = sb("picked_sc", [P, H + S], U8, tag="picked_then_late")
+        picked2_sc = sb("picked2_sc", [P, S], U8)
+        w_sc = sb("w_sc", [P, 2 * N], U8)
+        placed_late_sc = sb("placed_late_sc", [P, S + 2 * N], U8)
+        placed_sc = sb("placed_sc", [P, H + S], U8)
 
         nc.vector.memset(d_sc[:].bitcast(I32), 0)
-        nc.vector.memset(x_sc[:].bitcast(I32), 0)
-        nc.gpsimd.memset(placed_sc[:].bitcast(I32), 0)
+        nc.gpsimd.memset(x_sc[:].bitcast(I32), 0)
+        nc.vector.memset(placed_sc[:].bitcast(I32), 0)
+        nc.vector.memset(placed_late_sc[:].bitcast(I32), 0)
+        nc.gpsimd.memset(w_sc[:].bitcast(I32), 0)
 
         nc.gpsimd.dma_start(gain[:], gn.rearrange("(p t) o -> p (t o)", t=PACK))
+        nc.gpsimd.dma_start(w_sc[0:P:8, 0:N].bitcast(I32), w1_scales[0].bitcast(I32))
+        nc.gpsimd.dma_start(w_sc[0:P:8, N:].bitcast(I32), w2_scales[0].bitcast(I32))
         nc.scalar.dma_start(d_sc[0:P:8, :].bitcast(I32), d_scales[0].bitcast(I32))
         nc.scalar.dma_start(x_sc[0:P:8, :].bitcast(I32), x_scales[0].bitcast(I32))
         for list_t, source in ((k1_t, k1), (offs_t, offs), (two_t, two), (n1_t, n1), (n2_t, n2)):
             nc.sync.dma_start(list_t[:], source)
-        nc.sync.dma_start(d_w[:].bitcast(I32), words_in_hbm(d_words))
         nc.sync.dma_start(x_w[:].bitcast(I32), words_in_hbm(x_words))
+        nc.sync.dma_start(d_w[:].bitcast(I32), words_in_hbm(d_words))
         nc.sync.dma_start(n3_t[:], n3)
         nc.sync.dma_start(n4_t[:], n4)
 
         nc.vector.tensor_copy(picked_sc[:, 0:H], d_sc[:].indirect(k1_t[:]))
         nc.vector.tensor_copy(picked_sc[:, H : H + S], x_sc[:].indirect(offs_t[:]))
-        nc.vector.tensor_copy(picked_sc[:, H + S :], x_sc[:].indirect(two_t[:]))
         for r in range(4):
-            queue = nc.scalar if r % 2 else nc.sync
+            queue = nc.scalar if r == 3 else nc.sync
             queue.dma_start(placed_sc[r:P:32, :].bitcast(I32), picked_sc[8 * r : P : 32, :].bitcast(I32))
+        nc.vector.tensor_copy(picked2_sc[:], x_sc[:].indirect(two_t[:]))
+        warm = sb("warm", [P, 1], F32)
+        nc.scalar.activation(warm[:], gain[:, 0:1], ACT.Sigmoid)
 
         picked_w = sb("picked_w", [P, H + 2 * S], U32, tag="x_sc_then_words")
         d_picked, xq_w, x2_w = picked_w[:, 0:H], picked_w[:, H : H + S], picked_w[:, H + S :]
-        d_dealt, d_dealt_sc = sb("d_dealt", [P, H], U32), sb("d_dealt_sc", [P, H], U8)
-        nc.vector.tensor_copy(d_picked, d_w[:].indirect(k1_t[:]))
+        d_dealt, d_dealt_sc = sb("d_dealt", [P, H], U32, tag="dealt_words"), sb("d_dealt_sc", [P, H], U8)
         nc.vector.tensor_copy(xq_w, x_w[:].indirect(offs_t[:]))
+        nc.vector.tensor_copy(d_picked, d_w[:].indirect(k1_t[:]))
         nc.vector.tensor_copy(
-            d_dealt[:].bitcast(I32).rearrange("p (t m) -> p t m", t=PACK),
-            d_picked.bitcast(I32).rearrange("p (m t) -> p t m", t=PACK),
+            d_dealt[:].bitcast(I32).rearrange("p (t m) -> p m t", t=PACK),
+            d_picked.bitcast(I32).rearrange("p (m t) -> p m t", t=PACK),
         )
-        for u in range(2):
-            nc.vector.tensor_copy(
-                d_dealt_sc[:].rearrange("p (t m) -> p t m", t=PACK)[:, 2 * u : 2 * u + 2, :],
-                placed_sc[:, 0:H].rearrange("p (m t) -> p t m", t=PACK)[:, 2 * u : 2 * u + 2, :],
-            )
+        nc.vector.tensor_copy(
+            d_dealt_sc[:].rearrange("p (t m) -> p m t", t=PACK),
+            placed_sc[:, 0:H].rearrange("p (m t) -> p m t", t=PACK),
+        )
 
         w_w = sb("w_w", [P, 2 * N], U32, tag="d_w_then_w_w")
         nc.sync.dma_start(w_w[:, N:].bitcast(I32), words_in_hbm(w2_words))
         nc.sync.dma_start(w_w[:, 0:N].bitcast(I32), words_in_hbm(w1_words))
-        w_sc = sb("w_sc", [P, N], U8, tag="picked_then_w_sc")
-        nc.gpsimd.memset(w_sc[:].bitcast(I32), 0)
-        for which, scales in enumerate((w1_scales, w2_scales)):
-            for q in range(4):
-                first = 32 * q + 4 * which
-                nc.sync.dma_start(
-                    w_sc[first : first + 4, :].bitcast(I32), scales[0, 4 * q : 4 * q + 4, :].bitcast(I32)
-                )
+        late_sc = sb("late_sc", [P, S + 2 * N], U8, tag="picked_then_late")
+        nc.vector.tensor_copy(late_sc[:, 0:S].bitcast(I32), picked2_sc[:].bitcast(I32))
+        nc.vector.tensor_copy(
+            late_sc[:, S:].rearrange("p (w t m) -> p w m t", w=2, t=PACK),
+            w_sc[:].rearrange("p (w m t) -> p w m t", w=2, t=PACK),
+        )
+        for r in range(4):
+            nc.sync.dma_start(placed_late_sc[r:P:32, :].bitcast(I32), late_sc[8 * r : P : 32, :].bitcast(I32))
 
         h_ps = [psum.tile([P, S], F32, name="h_ps%d" % t) for t in range(PACK)]
         h2_ps = [psum.tile([P, S], F32, name="h2_ps%d" % t) for t in range(PACK)]
@@ -109,63 +117,55 @@ def tile_picked_pqmixfillhopd_none_po_kernel(
 
         ds = [sb("ds%d" % t, [P, S], F32) for t in range(PACK)]
         ra = [sb("ra%d" % t, [P, W], F32) for t in range(PACK)]
+        h2 = [sb("h2_%d" % t, [P, 2 * S], F32) for t in range(PACK)]
         for t in range(PACK):
-            pa, pb = sb("pa%d" % t, [P, W], F32), sb("pb%d" % t, [P, W], F32)
+            pa, pb = h2[t][:, S : S + W], h2[t][:, S + W :]
             if t == 0:
                 nc.scalar.copy(ds[t][:], h_ps[t][:])
             else:
                 nc.vector.tensor_copy(ds[t][:], h_ps[t][:])
-            nc.scalar.activation(pa[:], ds[t][:].indirect(n1_t[:]), ACT.Copy)
-            nc.vector.tensor_copy(pb[:], ds[t][:].indirect(n2_t[:]))
-            nc.vector.tensor_tensor(ra[t][:], pa[:], pb[:], ALU.max)
+            nc.scalar.activation(pa, ds[t][:].indirect(n1_t[:]), ACT.Copy)
+            nc.vector.tensor_copy(pb, ds[t][:].indirect(n2_t[:]))
+            nc.vector.tensor_tensor(ra[t][:], pa, pb, ALU.max)
         for t in range(PACK):
             nc.scalar.activation(ds[t][:].indirect(n1_t[:]), ra[t][:], ACT.Copy)
         nc.vector.tensor_copy(x2_w, x_w[:].indirect(two_t[:]))
-        w_dealt, w_dealt_sc = sb("w_dealt", [P, 2 * N], U32), sb("w_dealt_sc", [P, N], U8)
+        w_dealt = sb("w_dealt", [P, 2 * N], U32, tag="dealt_words")
         for first in (N, 0):
             nc.vector.tensor_copy(
-                w_dealt[:, first : first + N].bitcast(I32).rearrange("p (t m) -> p t m", t=PACK),
-                w_w[:, first : first + N].bitcast(I32).rearrange("p (m t) -> p t m", t=PACK),
+                w_dealt[:, first : first + N].bitcast(I32).rearrange("p (t m) -> p m t", t=PACK),
+                w_w[:, first : first + N].bitcast(I32).rearrange("p (m t) -> p m t", t=PACK),
             )
-        nc.vector.tensor_copy(
-            w_dealt_sc[:].rearrange("p (t m) -> p t m", t=PACK),
-            w_sc[:].rearrange("p (m t) -> p t m", t=PACK),
-        )
 
-        z_bf = sb("z_bf", [P, S, PACK], BF16, tag="picked_then_w_sc")
+        z_bf = sb("z_bf", [P, S, PACK], BF16, tag="d_w_then_w_w")
         for t in range(PACK):
             nc.vector.tensor_scalar(z_bf[:, :, t], ds[t][:], gain[:, t : t + 1], 0.0625, ALU.mult, ALU.mult)
 
         z_w, z_sc = sb("z_w", [P, S], U32), sb("z_sc", [P, S], U8)
-        nc.gpsimd.memset(z_sc[:].bitcast(I32), 0)
         nc.vector.quantize_mx(out=z_w[:].bitcast(FP8X4), scales=z_sc[:], in_=z_bf[:].rearrange("p j t -> p (j t)"))
 
         for t in range(PACK):
             cols = slice(P * t, P * (t + 1))
             nc.tensor.matmul_mx(
                 out=h2_ps[t][:], lhsT=w_dealt[:, N + P * t : N + P * (t + 1)].bitcast(FP8X4),
-                lhsT_scale=w_dealt_sc[4:P, cols],
-                rhs=x2_w.bitcast(FP8X4), rhs_scale=placed_sc[:, H + S :], start=True, stop=False,
+                lhsT_scale=placed_late_sc[:, S + N + P * t : S + N + P * (t + 1)],
+                rhs=x2_w.bitcast(FP8X4), rhs_scale=placed_late_sc[:, 0:S], start=True, stop=False,
             )
         for t in range(PACK):
             cols = slice(P * t, P * (t + 1))
             nc.tensor.matmul_mx(
-                out=h2_ps[t][:], lhsT=w_dealt[:, cols].bitcast(FP8X4), lhsT_scale=w_dealt_sc[:, cols],
+                out=h2_ps[t][:], lhsT=w_dealt[:, cols].bitcast(FP8X4), lhsT_scale=placed_late_sc[:, S + P * t : S + P * (t + 1)],
                 rhs=z_w[:].bitcast(FP8X4), rhs_scale=z_sc[:], start=False, stop=True,
             )
 
-        st = []
+        st = [sb("st%d" % t, [P, 2 * S], F32) for t in range(PACK)]
         for t in range(PACK):
-            h2, g3 = sb("h2_%d" % t, [P, 2 * S], F32), sb("g3_%d" % t, [P, S], F32)
-            st.append(sb("st%d" % t, [P, 2 * S], F32))
-            nc.gpsimd.memset(h2[:, S:], 0.0)
-            nc.gpsimd.memset(st[t][:, S:], 0.0)
             if t == 0:
-                nc.scalar.copy(h2[:, 0:S], h2_ps[t][:])
+                nc.scalar.copy(h2[t][:, 0:S], h2_ps[t][:])
             else:
-                nc.vector.tensor_copy(h2[:, 0:S], h2_ps[t][:])
-            nc.scalar.activation(g3[:], h2[:].indirect(n3_t[:]), ACT.Copy)
-            nc.vector.tensor_tensor(st[t][:, 0:S], g3[:], h2_ps[t][:], ALU.subtract)
+                nc.vector.tensor_copy(h2[t][:, 0:S], h2_ps[t][:])
+            nc.scalar.activation(st[t][:, S:], h2[t][:].indirect(n3_t[:]), ACT.Copy)
+            nc.vector.tensor_tensor(st[t][:, 0:S], st[t][:, S:], h2_ps[t][:], ALU.subtract)
 
         o_w, o_sc = sb("o_w", [P, S], U32), sb("o_sc", [P, S], U8)
         out_rows = out_0.rearrange("(p t) j -> p t j", t=PACK)

@@ -47,8 +47,9 @@ def tile_picked_pqmixfillhopd_none_po_kernel(
         d_sc, x_sc = sb("d_sc", [P, G], U8), sb("x_sc", [P, T], U8, tag="x_sc_then_words")
         d_w, x_w = sb("d_w", [P, G], U32, tag="d_w_then_w_w"), sb("x_w", [P, T], U32)
         gain = sb("gain", [P, PACK], F32)
-        picked_sc = sb("picked_sc", [P, H + S], U8, tag="picked_then_late")
-        picked2_sc = sb("picked2_sc", [P, S], U8)
+        picked_sc = sb("picked_sc", [P, H + S], U8)
+        early_sc = sb("early_sc", [P, H + S], U8, tag="early_then_late")
+        picked2_sc = sb("picked2_sc", [P, S], U8, tag="x2_sc_then_words")
         w_sc = sb("w_sc", [P, 2 * N], U8)
         placed_late_sc = sb("placed_late_sc", [P, S + 2 * N], U8)
         placed_sc = sb("placed_sc", [P, H + S], U8)
@@ -72,32 +73,33 @@ def tile_picked_pqmixfillhopd_none_po_kernel(
         nc.sync.dma_start(n4_t[:], n4)
 
         nc.vector.tensor_copy(picked_sc[:, 0:H], d_sc[:].indirect(k1_t[:]))
-        nc.vector.tensor_copy(picked_sc[:, H : H + S], x_sc[:].indirect(offs_t[:]))
+        nc.vector.tensor_copy(
+            early_sc[:, 0:H].rearrange("p (t m) -> p m t", t=PACK),
+            picked_sc[:, 0:H].rearrange("p (m t) -> p m t", t=PACK),
+        )
+        nc.vector.tensor_copy(picked_sc[:, H:], x_sc[:].indirect(offs_t[:]))
+        nc.vector.tensor_copy(early_sc[:, H:].bitcast(I32), picked_sc[:, H:].bitcast(I32))
         for r in range(4):
             queue = nc.scalar if r == 3 else nc.sync
-            queue.dma_start(placed_sc[r:P:32, :].bitcast(I32), picked_sc[8 * r : P : 32, :].bitcast(I32))
+            queue.dma_start(placed_sc[r:P:32, :].bitcast(I32), early_sc[8 * r : P : 32, :].bitcast(I32))
         nc.vector.tensor_copy(picked2_sc[:], x_sc[:].indirect(two_t[:]))
         warm = sb("warm", [P, 1], F32)
         nc.scalar.activation(warm[:], gain[:, 0:1], ACT.Sigmoid)
 
-        picked_w = sb("picked_w", [P, H + 2 * S], U32, tag="x_sc_then_words")
-        d_picked, xq_w, x2_w = picked_w[:, 0:H], picked_w[:, H : H + S], picked_w[:, H + S :]
-        d_dealt, d_dealt_sc = sb("d_dealt", [P, H], U32, tag="dealt_words"), sb("d_dealt_sc", [P, H], U8)
+        picked_w = sb("picked_w", [P, H + S], U32, tag="x_sc_then_words")
+        d_picked, xq_w = picked_w[:, 0:H], picked_w[:, H:]
+        d_dealt = sb("d_dealt", [P, H], U32, tag="dealt_words")
         nc.vector.tensor_copy(xq_w, x_w[:].indirect(offs_t[:]))
         nc.vector.tensor_copy(d_picked, d_w[:].indirect(k1_t[:]))
         nc.vector.tensor_copy(
             d_dealt[:].bitcast(I32).rearrange("p (t m) -> p m t", t=PACK),
             d_picked.bitcast(I32).rearrange("p (m t) -> p m t", t=PACK),
         )
-        nc.vector.tensor_copy(
-            d_dealt_sc[:].rearrange("p (t m) -> p m t", t=PACK),
-            placed_sc[:, 0:H].rearrange("p (m t) -> p m t", t=PACK),
-        )
 
         w_w = sb("w_w", [P, 2 * N], U32, tag="d_w_then_w_w")
         nc.sync.dma_start(w_w[:, N:].bitcast(I32), words_in_hbm(w2_words))
         nc.sync.dma_start(w_w[:, 0:N].bitcast(I32), words_in_hbm(w1_words))
-        late_sc = sb("late_sc", [P, S + 2 * N], U8, tag="picked_then_late")
+        late_sc = sb("late_sc", [P, S + 2 * N], U8, tag="early_then_late")
         nc.vector.tensor_copy(late_sc[:, 0:S].bitcast(I32), picked2_sc[:].bitcast(I32))
         nc.vector.tensor_copy(
             late_sc[:, S:].rearrange("p (w t m) -> p w m t", w=2, t=PACK),
@@ -111,7 +113,7 @@ def tile_picked_pqmixfillhopd_none_po_kernel(
         for t in range(PACK):
             cols = slice(P * t, P * (t + 1))
             nc.tensor.matmul_mx(
-                out=h_ps[t][:], lhsT=d_dealt[:, cols].bitcast(FP8X4), lhsT_scale=d_dealt_sc[:, cols],
+                out=h_ps[t][:], lhsT=d_dealt[:, cols].bitcast(FP8X4), lhsT_scale=placed_sc[:, cols],
                 rhs=xq_w.bitcast(FP8X4), rhs_scale=placed_sc[:, H : H + S], start=True, stop=True,
             )
 
@@ -129,7 +131,8 @@ def tile_picked_pqmixfillhopd_none_po_kernel(
             nc.vector.tensor_tensor(ra[t][:], pa, pb, ALU.max)
         for t in range(PACK):
             nc.scalar.activation(ds[t][:].indirect(n1_t[:]), ra[t][:], ACT.Copy)
-        nc.vector.tensor_copy(x2_w, x_w[:].indirect(two_t[:]))
+        x2_w = sb("x2_w", [P, S], U32, tag="x2_sc_then_words")
+        nc.vector.tensor_copy(x2_w[:], x_w[:].indirect(two_t[:]))
         w_dealt = sb("w_dealt", [P, 2 * N], U32, tag="dealt_words")
         for first in (N, 0):
             nc.vector.tensor_copy(
@@ -138,18 +141,26 @@ def tile_picked_pqmixfillhopd_none_po_kernel(
             )
 
         z_bf = sb("z_bf", [P, S, PACK], BF16, tag="d_w_then_w_w")
+        halves = [slice(0, HALF), slice(HALF, S)]
         for t in range(PACK):
-            nc.vector.tensor_scalar(z_bf[:, :, t], ds[t][:], gain[:, t : t + 1], 0.0625, ALU.mult, ALU.mult)
+            for cols in halves if t == PACK - 1 else [slice(0, S)]:
+                nc.vector.tensor_scalar(
+                    z_bf[:, cols, t], ds[t][:, cols], gain[:, t : t + 1], 0.0625, ALU.mult, ALU.mult
+                )
 
         z_w, z_sc = sb("z_w", [P, S], U32), sb("z_sc", [P, S], U8)
-        nc.vector.quantize_mx(out=z_w[:].bitcast(FP8X4), scales=z_sc[:], in_=z_bf[:].rearrange("p j t -> p (j t)"))
+        for cols in halves:
+            nc.vector.quantize_mx(
+                out=z_w[:, cols].bitcast(FP8X4), scales=z_sc[:, cols],
+                in_=z_bf[:, cols, :].rearrange("p j t -> p (j t)"),
+            )
 
         for t in range(PACK):
             cols = slice(P * t, P * (t + 1))
             nc.tensor.matmul_mx(
                 out=h2_ps[t][:], lhsT=w_dealt[:, N + P * t : N + P * (t + 1)].bitcast(FP8X4),
                 lhsT_scale=placed_late_sc[:, S + N + P * t : S + N + P * (t + 1)],
-                rhs=x2_w.bitcast(FP8X4), rhs_scale=placed_late_sc[:, 0:S], start=True, stop=False,
+                rhs=x2_w[:].bitcast(FP8X4), rhs_scale=placed_late_sc[:, 0:S], start=True, stop=False,
             )
         for t in range(PACK):
             cols = slice(P * t, P * (t + 1))

@@ -5,7 +5,11 @@ import concourse.mybir as mybir
 K, T, S, N, G, H, W = 512, 1024, 256, 512, 2048, 512, 128
 P = 128
 PACK = 4
+QUADRANTS = 4
 HALF = S // 2
+HALVES = (slice(0, HALF), slice(HALF, S))
+WHOLE = slice(0, S)
+LIST_ROWS = 16
 
 F32 = mybir.dt.float32
 BF16 = mybir.dt.bfloat16
@@ -29,6 +33,11 @@ def tile_picked_pqmixfillhopd_none_po_kernel(
     def words_in_hbm(words):
         return words[0].rearrange("p n t -> p (n t)").bitcast(I32)
 
+    def deal(dealt, plain):
+        nc.vector.tensor_copy(
+            dealt.rearrange("p (t m) -> p m t", t=PACK), plain.rearrange("p (m t) -> p m t", t=PACK)
+        )
+
     with ExitStack() as ctx:
         lists = ctx.enter_context(tc.tile_pool(name="lists", bufs=1))
         keep = ctx.enter_context(tc.tile_pool(name="keep", bufs=1))
@@ -44,76 +53,69 @@ def tile_picked_pqmixfillhopd_none_po_kernel(
         n1_t, n2_t = list_tile("n1_t", n1), list_tile("n2_t", n2)
         n3_t, n4_t = list_tile("n3_t", n3), list_tile("n4_t", n4)
 
-        d_sc, x_sc = sb("d_sc", [P, G], U8), sb("x_sc", [P, T], U8, tag="x_sc_then_words")
-        d_w, x_w = sb("d_w", [P, G], U32, tag="d_w_then_w_w"), sb("x_w", [P, T], U32)
+        d_sc, x_sc = sb("d_sc", [P, G], U8, tag="d_sc_then_x2"), sb("x_sc", [P, T], U8)
+        d_w, x_w = sb("d_w", [P, G], U32, tag="d_w_then_w_then_z"), sb("x_w", [P, T], U32)
         gain = sb("gain", [P, PACK], F32)
-        picked_sc = sb("picked_sc", [P, H + S], U8)
+        picked_sc = sb("picked_sc", [P, H + S], U8, tag="picked_sc_then_words")
         early_sc = sb("early_sc", [P, H + S], U8, tag="early_then_late")
-        picked2_sc = sb("picked2_sc", [P, S], U8, tag="x2_sc_then_words")
-        w_sc = sb("w_sc", [P, 2 * N], U8)
-        placed_late_sc = sb("placed_late_sc", [P, S + 2 * N], U8)
+        w_sc = sb("w_sc", [P, N], U8)
+        placed_late_sc = sb("placed_late_sc", [P, S + N], U8)
         placed_sc = sb("placed_sc", [P, H + S], U8)
 
+        warm_in, warm_out = sb("warm_in", [P, 1], F32), sb("warm_out", [P, 1], F32)
         nc.vector.memset(d_sc[:].bitcast(I32), 0)
         nc.gpsimd.memset(x_sc[:].bitcast(I32), 0)
         nc.vector.memset(placed_sc[:].bitcast(I32), 0)
         nc.vector.memset(placed_late_sc[:].bitcast(I32), 0)
-        nc.gpsimd.memset(w_sc[:].bitcast(I32), 0)
+        nc.vector.memset(w_sc[:].bitcast(I32), 0)
+        nc.vector.memset(warm_in[:], 0.0)
 
-        nc.gpsimd.dma_start(gain[:], gn.rearrange("(p t) o -> p (t o)", t=PACK))
-        nc.gpsimd.dma_start(w_sc[0:P:8, 0:N].bitcast(I32), w1_scales[0].bitcast(I32))
-        nc.gpsimd.dma_start(w_sc[0:P:8, N:].bitcast(I32), w2_scales[0].bitcast(I32))
         nc.scalar.dma_start(d_sc[0:P:8, :].bitcast(I32), d_scales[0].bitcast(I32))
-        nc.scalar.dma_start(x_sc[0:P:8, :].bitcast(I32), x_scales[0].bitcast(I32))
-        for list_t, source in ((k1_t, k1), (offs_t, offs), (two_t, two), (n1_t, n1), (n2_t, n2)):
+        nc.sync.dma_start(x_sc[0:P:8, :].bitcast(I32), x_scales[0].bitcast(I32))
+        for list_t, source in ((offs_t, offs), (k1_t, k1), (two_t, two), (n1_t, n1), (n2_t, n2)):
             nc.sync.dma_start(list_t[:], source)
         nc.sync.dma_start(x_w[:].bitcast(I32), words_in_hbm(x_words))
         nc.sync.dma_start(d_w[:].bitcast(I32), words_in_hbm(d_words))
         nc.sync.dma_start(n3_t[:], n3)
         nc.sync.dma_start(n4_t[:], n4)
+        nc.sync.dma_start(gain[:], gn.rearrange("(p t) o -> p (t o)", t=PACK))
+        nc.gpsimd.dma_start(w_sc[0:P:8, :].bitcast(I32), w1_scales[0].bitcast(I32))
+        nc.gpsimd.dma_start(w_sc[4:P:8, :].bitcast(I32), w2_scales[0].bitcast(I32))
+        nc.scalar.activation(warm_out[:], warm_in[:], ACT.Sigmoid)
 
-        nc.vector.tensor_copy(picked_sc[:, 0:H], d_sc[:].indirect(k1_t[:]))
-        nc.vector.tensor_copy(
-            early_sc[:, 0:H].rearrange("p (t m) -> p m t", t=PACK),
-            picked_sc[:, 0:H].rearrange("p (m t) -> p m t", t=PACK),
-        )
         nc.vector.tensor_copy(picked_sc[:, H:], x_sc[:].indirect(offs_t[:]))
+        nc.vector.tensor_copy(picked_sc[:, 0:H], d_sc[:].indirect(k1_t[:]))
         nc.vector.tensor_copy(early_sc[:, H:].bitcast(I32), picked_sc[:, H:].bitcast(I32))
+        deal(early_sc[:, 0:H], picked_sc[:, 0:H])
         for r in range(4):
-            queue = nc.scalar if r == 3 else nc.sync
-            queue.dma_start(placed_sc[r:P:32, :].bitcast(I32), early_sc[8 * r : P : 32, :].bitcast(I32))
-        nc.vector.tensor_copy(picked2_sc[:], x_sc[:].indirect(two_t[:]))
-        warm = sb("warm", [P, 1], F32)
-        nc.scalar.activation(warm[:], gain[:, 0:1], ACT.Sigmoid)
+            nc.sync.dma_start(placed_sc[r:P:32, :].bitcast(I32), early_sc[8 * r : P : 32, :].bitcast(I32))
 
-        picked_w = sb("picked_w", [P, H + S], U32, tag="x_sc_then_words")
+        picked_w = sb("picked_w", [P, H + S], U32, tag="picked_sc_then_words")
         d_picked, xq_w = picked_w[:, 0:H], picked_w[:, H:]
         d_dealt = sb("d_dealt", [P, H], U32, tag="dealt_words")
         nc.vector.tensor_copy(xq_w, x_w[:].indirect(offs_t[:]))
         nc.vector.tensor_copy(d_picked, d_w[:].indirect(k1_t[:]))
-        nc.vector.tensor_copy(
-            d_dealt[:].bitcast(I32).rearrange("p (t m) -> p m t", t=PACK),
-            d_picked.bitcast(I32).rearrange("p (m t) -> p m t", t=PACK),
-        )
+        deal(d_dealt[:].bitcast(I32), d_picked.bitcast(I32))
 
-        w_w = sb("w_w", [P, 2 * N], U32, tag="d_w_then_w_w")
+        x2_sc = sb("x2_sc", [P, S], U8, tag="d_sc_then_x2")
+        nc.vector.tensor_copy(x2_sc[:], x_sc[:].indirect(two_t[:]))
+        w_w = sb("w_w", [P, 2 * N], U32, tag="d_w_then_w_then_z")
         nc.sync.dma_start(w_w[:, N:].bitcast(I32), words_in_hbm(w2_words))
         nc.sync.dma_start(w_w[:, 0:N].bitcast(I32), words_in_hbm(w1_words))
-        late_sc = sb("late_sc", [P, S + 2 * N], U8, tag="early_then_late")
-        nc.vector.tensor_copy(late_sc[:, 0:S].bitcast(I32), picked2_sc[:].bitcast(I32))
-        nc.vector.tensor_copy(
-            late_sc[:, S:].rearrange("p (w t m) -> p w m t", w=2, t=PACK),
-            w_sc[:].rearrange("p (w m t) -> p w m t", w=2, t=PACK),
-        )
+        late_sc = sb("late_sc", [P, S + N], U8, tag="early_then_late")
+        nc.vector.tensor_copy(late_sc[:, 0:S].bitcast(I32), x2_sc[:].bitcast(I32))
+        deal(late_sc[:, S:], w_sc[:])
         for r in range(4):
             nc.sync.dma_start(placed_late_sc[r:P:32, :].bitcast(I32), late_sc[8 * r : P : 32, :].bitcast(I32))
+            nc.sync.dma_start(
+                placed_late_sc[4 + r : P : 32, S:].bitcast(I32), late_sc[8 * r + 4 : P : 32, S:].bitcast(I32)
+            )
 
-        h_ps = [psum.tile([P, S], F32, name="h_ps%d" % t) for t in range(PACK)]
-        h2_ps = [psum.tile([P, S], F32, name="h2_ps%d" % t) for t in range(PACK)]
+        h_ps = [psum.tile([P, S], F32, name="h_ps%d" % t, tag="h_ps%d" % t) for t in range(PACK)]
         for t in range(PACK):
-            cols = slice(P * t, P * (t + 1))
+            rows = slice(P * t, P * (t + 1))
             nc.tensor.matmul_mx(
-                out=h_ps[t][:], lhsT=d_dealt[:, cols].bitcast(FP8X4), lhsT_scale=placed_sc[:, cols],
+                out=h_ps[t][:], lhsT=d_dealt[:, rows].bitcast(FP8X4), lhsT_scale=placed_sc[:, rows],
                 rhs=xq_w.bitcast(FP8X4), rhs_scale=placed_sc[:, H : H + S], start=True, stop=True,
             )
 
@@ -131,70 +133,70 @@ def tile_picked_pqmixfillhopd_none_po_kernel(
             nc.vector.tensor_tensor(ra[t][:], pa, pb, ALU.max)
         for t in range(PACK):
             nc.scalar.activation(ds[t][:].indirect(n1_t[:]), ra[t][:], ACT.Copy)
-        x2_w = sb("x2_w", [P, S], U32, tag="x2_sc_then_words")
+
+        x2_w = sb("x2_w", [P, S], U32, tag="d_sc_then_x2")
         nc.vector.tensor_copy(x2_w[:], x_w[:].indirect(two_t[:]))
         w_dealt = sb("w_dealt", [P, 2 * N], U32, tag="dealt_words")
         for first in (N, 0):
-            nc.vector.tensor_copy(
-                w_dealt[:, first : first + N].bitcast(I32).rearrange("p (t m) -> p m t", t=PACK),
-                w_w[:, first : first + N].bitcast(I32).rearrange("p (m t) -> p m t", t=PACK),
-            )
+            deal(w_dealt[:, first : first + N].bitcast(I32), w_w[:, first : first + N].bitcast(I32))
 
-        z_bf = sb("z_bf", [P, S, PACK], BF16, tag="d_w_then_w_w")
-        halves = [slice(0, HALF), slice(HALF, S)]
+        z_bf = sb("z_bf", [P, S, PACK], BF16, tag="d_w_then_w_then_z")
         for t in range(PACK):
-            for cols in halves if t == PACK - 1 else [slice(0, S)]:
+            for cols in HALVES if t == PACK - 1 else [WHOLE]:
                 nc.vector.tensor_scalar(
                     z_bf[:, cols, t], ds[t][:, cols], gain[:, t : t + 1], 0.0625, ALU.mult, ALU.mult
                 )
-
         z_w, z_sc = sb("z_w", [P, S], U32), sb("z_sc", [P, S], U8)
-        for cols in halves:
+        for cols in HALVES:
             nc.vector.quantize_mx(
                 out=z_w[:, cols].bitcast(FP8X4), scales=z_sc[:, cols],
                 in_=z_bf[:, cols, :].rearrange("p j t -> p (j t)"),
             )
 
-        for t in range(PACK):
-            cols = slice(P * t, P * (t + 1))
+        pieces = [(0, HALVES[0]), (0, HALVES[1])] + [(t, WHOLE) for t in range(1, PACK)]
+        h2_ps = [
+            psum.tile([P, cols.stop - cols.start], F32, name="h2_ps%d" % i, tag="h_ps0" if i == 0 else "h2_ps%d" % i)
+            for i, (t, cols) in enumerate(pieces)
+        ]
+        for i, (t, cols) in enumerate(pieces):
             nc.tensor.matmul_mx(
-                out=h2_ps[t][:], lhsT=w_dealt[:, N + P * t : N + P * (t + 1)].bitcast(FP8X4),
-                lhsT_scale=placed_late_sc[:, S + N + P * t : S + N + P * (t + 1)],
-                rhs=x2_w[:].bitcast(FP8X4), rhs_scale=placed_late_sc[:, 0:S], start=True, stop=False,
+                out=h2_ps[i][:], lhsT=w_dealt[:, N + P * t : N + P * (t + 1)].bitcast(FP8X4),
+                lhsT_scale=placed_late_sc[4:P, S + P * t : S + P * (t + 1)],
+                rhs=x2_w[:, cols].bitcast(FP8X4), rhs_scale=placed_late_sc[:, cols], start=True, stop=False,
             )
-        for t in range(PACK):
-            cols = slice(P * t, P * (t + 1))
+        for i, (t, cols) in enumerate(pieces):
             nc.tensor.matmul_mx(
-                out=h2_ps[t][:], lhsT=w_dealt[:, cols].bitcast(FP8X4), lhsT_scale=placed_late_sc[:, S + P * t : S + P * (t + 1)],
-                rhs=z_w[:].bitcast(FP8X4), rhs_scale=z_sc[:], start=False, stop=True,
+                out=h2_ps[i][:], lhsT=w_dealt[:, P * t : P * (t + 1)].bitcast(FP8X4),
+                lhsT_scale=placed_late_sc[:, S + P * t : S + P * (t + 1)],
+                rhs=z_w[:, cols].bitcast(FP8X4), rhs_scale=z_sc[:, cols], start=False, stop=True,
             )
+            if i == 0:
+                nc.scalar.copy(h2[t][:, cols], h2_ps[i][:])
+            else:
+                nc.vector.tensor_copy(h2[t][:, cols], h2_ps[i][:])
 
         st = [sb("st%d" % t, [P, 2 * S], F32) for t in range(PACK)]
         for t in range(PACK):
-            if t == 0:
-                nc.scalar.copy(h2[t][:, 0:S], h2_ps[t][:])
-            else:
-                nc.vector.tensor_copy(h2[t][:, 0:S], h2_ps[t][:])
             nc.scalar.activation(st[t][:, S:], h2[t][:].indirect(n3_t[:]), ACT.Copy)
-            nc.vector.tensor_tensor(st[t][:, 0:S], st[t][:, S:], h2_ps[t][:], ALU.subtract)
+            nc.vector.tensor_tensor(st[t][:, 0:S], st[t][:, S:], h2[t][:, 0:S], ALU.subtract)
 
         o_w, o_sc = sb("o_w", [P, S], U32), sb("o_sc", [P, S], U8)
         out_rows = out_0.rearrange("(p t) j -> p t j", t=PACK)
         out_words = out_1[0].rearrange("p n t -> p (n t)").bitcast(I32)
-        for u in range(2):
-            cols = slice(HALF * u, HALF * (u + 1))
+        for u, cols in enumerate(HALVES):
+            entries = n4_t[:, cols.start // LIST_ROWS : cols.stop // LIST_ROWS]
             res = sb("res%d" % u, [P, PACK, HALF], F32)
             res_bf = sb("res_bf%d" % u, [P, HALF, PACK], BF16)
             for t in range(PACK):
                 gate = sb("gate%d_%d" % (u, t), [P, HALF], F32)
-                nc.scalar.activation(gate[:], st[t][:].indirect(n4_t[:, 8 * u : 8 * u + 8]), ACT.Sigmoid)
-                nc.vector.tensor_tensor(res[:, t, :], gate[:], h2_ps[t][:, cols], ALU.mult)
+                nc.scalar.activation(gate[:], st[t][:].indirect(entries), ACT.Sigmoid)
+                nc.vector.tensor_tensor(res[:, t, :], gate[:], h2[t][:, cols], ALU.mult)
             nc.sync.dma_start(out_rows[:, :, cols], res[:])
             nc.vector.tensor_copy(res_bf[:], res[:].rearrange("p t j -> p j t"))
             nc.vector.quantize_mx(
                 out=o_w[:, cols].bitcast(FP8X4), scales=o_sc[:, cols], in_=res_bf[:].rearrange("p j t -> p (j t)")
             )
             nc.sync.dma_start(out_words[:, cols], o_w[:, cols].bitcast(I32))
-        for q in range(4):
+        for q in range(QUADRANTS):
             queue = nc.scalar if q % 2 else nc.sync
             queue.dma_start(out_2[0, 4 * q : 4 * q + 4, :].bitcast(I32), o_sc[32 * q : 32 * q + 4, :].bitcast(I32))

from contextlib import ExitStack

import concourse.mybir as mybir

K, T, S, N, G, H, W = 512, 1024, 256, 512, 2048, 512, 128
P = 128
PACK = 4
QUADRANTS = 4
HALF = S // 2
HALVES = (slice(0, HALF), slice(HALF, S))
WHOLE = slice(0, S)
LIST_ROWS = 16

F32 = mybir.dt.float32
BF16 = mybir.dt.bfloat16
I32 = mybir.dt.int32
U32 = mybir.dt.uint32
U16 = mybir.dt.uint16
U8 = mybir.dt.uint8
FP8X4 = mybir.dt.float8_e4m3fn_x4
ALU = mybir.AluOpType
ACT = mybir.ActivationFunctionType

FLOPS = 2 * K * H * S + 2 * H * N * S + 2 * K * N * S


def tile_picked_pqmixfillhopd_none_po_kernel(
    tc, x_words, x_scales, d_words, d_scales, gn, w1_words, w1_scales, w2_words, w2_scales,
    offs, k1, n1, n2, two, n3, n4, out_0, out_1, out_2,
):
    nc = tc.nc

    def words_in_hbm(words):
        return words[0].rearrange("p n t -> p (n t)").bitcast(I32)

    def deal(dealt, plain):
        nc.vector.tensor_copy(
            dealt.rearrange("p (t m) -> p m t", t=PACK), plain.rearrange("p (m t) -> p m t", t=PACK)
        )

    with ExitStack() as ctx:
        lists = ctx.enter_context(tc.tile_pool(name="lists", bufs=1))
        keep = ctx.enter_context(tc.tile_pool(name="keep", bufs=1))
        psum = ctx.enter_context(tc.psum_pool(name="psum", bufs=1))

        def list_tile(name, source):
            return lists.tile(list(source.shape), U16, name=name)

        def sb(name, shape, dtype, tag=None):
            return keep.tile(shape, dtype, name=name, tag=tag or name, align_bytes=64)

        k1_t, offs_t, two_t = list_tile("k1_t", k1), list_tile("offs_t", offs), list_tile("two_t", two)
        n1_t, n2_t = list_tile("n1_t", n1), list_tile("n2_t", n2)
        n3_t, n4_t = list_tile("n3_t", n3), list_tile("n4_t", n4)

        d_sc, x_sc = sb("d_sc", [P, G], U8, tag="d_sc_then_x2"), sb("x_sc", [P, T], U8)
        d_w, x_w = sb("d_w", [P, G], U32, tag="d_w_then_w_then_z"), sb("x_w", [P, T], U32)
        gain = sb("gain", [P, PACK], F32)
        picked_sc = sb("picked_sc", [P, H + S], U8, tag="picked_sc_then_words")
        early_sc = sb("early_sc", [P, H + S], U8, tag="early_then_late")
        w_sc = sb("w_sc", [P, N], U8)
        placed_late_sc = sb("placed_late_sc", [P, S + N], U8)
        placed_sc = sb("placed_sc", [P, H + S], U8)

        warm_in, warm_out = sb("warm_in", [P, 1], F32), sb("warm_out", [P, 1], F32)
        nc.vector.memset(d_sc[:].bitcast(I32), 0)
        nc.gpsimd.memset(x_sc[:].bitcast(I32), 0)
        nc.vector.memset(placed_sc[:].bitcast(I32), 0)
        nc.vector.memset(placed_late_sc[:].bitcast(I32), 0)
        nc.vector.memset(w_sc[:].bitcast(I32), 0)
        nc.vector.memset(warm_in[:], 0.0)

        nc.scalar.dma_start(d_sc[0:P:8, :].bitcast(I32), d_scales[0].bitcast(I32))
        nc.sync.dma_start(x_sc[0:P:8, :].bitcast(I32), x_scales[0].bitcast(I32))
        for list_t, source in ((offs_t, offs), (k1_t, k1), (two_t, two), (n1_t, n1), (n2_t, n2)):
            nc.sync.dma_start(list_t[:], source)
        nc.sync.dma_start(x_w[:].bitcast(I32), words_in_hbm(x_words))
        nc.sync.dma_start(d_w[:].bitcast(I32), words_in_hbm(d_words))
        nc.sync.dma_start(n3_t[:], n3)
        nc.sync.dma_start(n4_t[:], n4)
        nc.sync.dma_start(gain[:], gn.rearrange("(p t) o -> p (t o)", t=PACK))
        nc.gpsimd.dma_start(w_sc[0:P:8, :].bitcast(I32), w1_scales[0].bitcast(I32))
        nc.gpsimd.dma_start(w_sc[4:P:8, :].bitcast(I32), w2_scales[0].bitcast(I32))
        nc.scalar.activation(warm_out[:], warm_in[:], ACT.Sigmoid)

        nc.vector.tensor_copy(picked_sc[:, H:], x_sc[:].indirect(offs_t[:]))
        nc.vector.tensor_copy(picked_sc[:, 0:H], d_sc[:].indirect(k1_t[:]))
        nc.vector.tensor_copy(early_sc[:, H:].bitcast(I32), picked_sc[:, H:].bitcast(I32))
        deal(early_sc[:, 0:H], picked_sc[:, 0:H])
        for r in range(4):
            nc.sync.dma_start(placed_sc[r:P:32, :].bitcast(I32), early_sc[8 * r : P : 32, :].bitcast(I32))

        picked_w = sb("picked_w", [P, H + S], U32, tag="picked_sc_then_words")
        d_picked, xq_w = picked_w[:, 0:H], picked_w[:, H:]
        d_dealt = sb("d_dealt", [P, H], U32, tag="dealt_words")
        nc.vector.tensor_copy(xq_w, x_w[:].indirect(offs_t[:]))
        nc.vector.tensor_copy(d_picked, d_w[:].indirect(k1_t[:]))
        deal(d_dealt[:].bitcast(I32), d_picked.bitcast(I32))

        x2_sc = sb("x2_sc", [P, S], U8, tag="d_sc_then_x2")
        nc.vector.tensor_copy(x2_sc[:], x_sc[:].indirect(two_t[:]))
        w_w = sb("w_w", [P, 2 * N], U32, tag="d_w_then_w_then_z")
        nc.sync.dma_start(w_w[:, N:].bitcast(I32), words_in_hbm(w2_words))
        nc.sync.dma_start(w_w[:, 0:N].bitcast(I32), words_in_hbm(w1_words))
        late_sc = sb("late_sc", [P, S + N], U8, tag="early_then_late")
        nc.vector.tensor_copy(late_sc[:, 0:S].bitcast(I32), x2_sc[:].bitcast(I32))
        deal(late_sc[:, S:], w_sc[:])
        for r in range(4):
            nc.sync.dma_start(placed_late_sc[r:P:32, :].bitcast(I32), late_sc[8 * r : P : 32, :].bitcast(I32))
            nc.sync.dma_start(
                placed_late_sc[4 + r : P : 32, S:].bitcast(I32), late_sc[8 * r + 4 : P : 32, S:].bitcast(I32)
            )

        h_ps = [psum.tile([P, S], F32, name="h_ps%d" % t, tag="h_ps%d" % t) for t in range(PACK)]
        for t in range(PACK):
            rows = slice(P * t, P * (t + 1))
            nc.tensor.matmul_mx(
                out=h_ps[t][:], lhsT=d_dealt[:, rows].bitcast(FP8X4), lhsT_scale=placed_sc[:, rows],
                rhs=xq_w.bitcast(FP8X4), rhs_scale=placed_sc[:, H : H + S], start=True, stop=True,
            )

        ds = [sb("ds%d" % t, [P, S], F32) for t in range(PACK)]
        ra = [sb("ra%d" % t, [P, W], F32) for t in range(PACK)]
        h2 = [sb("h2_%d" % t, [P, 2 * S], F32) for t in range(PACK)]
        for t in range(PACK):
            pa, pb = h2[t][:, S : S + W], h2[t][:, S + W :]
            if t == 0:
                nc.scalar.copy(ds[t][:], h_ps[t][:])
            else:
                nc.vector.tensor_copy(ds[t][:], h_ps[t][:])
            nc.scalar.activation(pa, ds[t][:].indirect(n1_t[:]), ACT.Copy)
            nc.vector.tensor_copy(pb, ds[t][:].indirect(n2_t[:]))
            nc.vector.tensor_tensor(ra[t][:], pa, pb, ALU.max)
        for t in range(PACK):
            nc.scalar.activation(ds[t][:].indirect(n1_t[:]), ra[t][:], ACT.Copy)

        x2_w = sb("x2_w", [P, S], U32, tag="d_sc_then_x2")
        nc.vector.tensor_copy(x2_w[:], x_w[:].indirect(two_t[:]))
        w_dealt = sb("w_dealt", [P, 2 * N], U32, tag="dealt_words")
        for first in (N, 0):
            deal(w_dealt[:, first : first + N].bitcast(I32), w_w[:, first : first + N].bitcast(I32))

        z_bf = sb("z_bf", [P, S, PACK], BF16, tag="d_w_then_w_then_z")
        for t in range(PACK):
            for cols in HALVES if t == PACK - 1 else [WHOLE]:
                nc.vector.tensor_scalar(
                    z_bf[:, cols, t], ds[t][:, cols], gain[:, t : t + 1], 0.0625, ALU.mult, ALU.mult
                )
        z_w, z_sc = sb("z_w", [P, S], U32), sb("z_sc", [P, S], U8)
        for cols in HALVES:
            nc.vector.quantize_mx(
                out=z_w[:, cols].bitcast(FP8X4), scales=z_sc[:, cols],
                in_=z_bf[:, cols, :].rearrange("p j t -> p (j t)"),
            )

        pieces = [(0, HALVES[0]), (0, HALVES[1])] + [(t, WHOLE) for t in range(1, PACK)]
        h2_ps = [
            psum.tile([P, cols.stop - cols.start], F32, name="h2_ps%d" % i, tag="h_ps0" if i == 0 else "h2_ps%d" % i)
            for i, (t, cols) in enumerate(pieces)
        ]
        for i, (t, cols) in enumerate(pieces):
            nc.tensor.matmul_mx(
                out=h2_ps[i][:], lhsT=w_dealt[:, N + P * t : N + P * (t + 1)].bitcast(FP8X4),
                lhsT_scale=placed_late_sc[4:P, S + P * t : S + P * (t + 1)],
                rhs=x2_w[:, cols].bitcast(FP8X4), rhs_scale=placed_late_sc[:, cols], start=True, stop=False,
            )
        for i, (t, cols) in enumerate(pieces):
            nc.tensor.matmul_mx(
                out=h2_ps[i][:], lhsT=w_dealt[:, P * t : P * (t + 1)].bitcast(FP8X4),
                lhsT_scale=placed_late_sc[:, S + P * t : S + P * (t + 1)],
                rhs=z_w[:, cols].bitcast(FP8X4), rhs_scale=z_sc[:, cols], start=False, stop=True,
            )
            if i == 0:
                nc.scalar.copy(h2[t][:, cols], h2_ps[i][:])
            else:
                nc.vector.tensor_copy(h2[t][:, cols], h2_ps[i][:])

        st = [sb("st%d" % t, [P, 2 * S], F32) for t in range(PACK)]
        for t in range(PACK):
            nc.scalar.activation(st[t][:, S:], h2[t][:].indirect(n3_t[:]), ACT.Copy)
            nc.vector.tensor_tensor(st[t][:, 0:S], st[t][:, S:], h2[t][:, 0:S], ALU.subtract)

        o_w, o_sc = sb("o_w", [P, S], U32), sb("o_sc", [P, S], U8)
        out_rows = out_0.rearrange("(p t) j -> p t j", t=PACK)
        out_words = out_1[0].rearrange("p n t -> p (n t)").bitcast(I32)
        for u, cols in enumerate(HALVES):
            entries = n4_t[:, cols.start // LIST_ROWS : cols.stop // LIST_ROWS]
            res = sb("res%d" % u, [P, PACK, HALF], F32)
            res_bf = sb("res_bf%d" % u, [P, HALF, PACK], BF16)
            for t in range(PACK):
                gate = sb("gate%d_%d" % (u, t), [P, HALF], F32)
                nc.scalar.activation(gate[:], st[t][:].indirect(entries), ACT.Sigmoid)
                nc.vector.tensor_tensor(res[:, t, :], gate[:], h2[t][:, cols], ALU.mult)
            nc.sync.dma_start(out_rows[:, :, cols], res[:])
            nc.vector.tensor_copy(res_bf[:], res[:].rearrange("p t j -> p j t"))
            nc.vector.quantize_mx(
                out=o_w[:, cols].bitcast(FP8X4), scales=o_sc[:, cols], in_=res_bf[:].rearrange("p j t -> p (j t)")
            )
            nc.sync.dma_start(out_words[:, cols], o_w[:, cols].bitcast(I32))
        for q in range(QUADRANTS):
            queue = nc.scalar if q % 2 else nc.sync
            queue.dma_start(out_2[0, 4 * q : 4 * q + 4, :].bitcast(I32), o_sc[32 * q : 32 * q + 4, :].bitcast(I32))
